import numpy as np
import ml_dtypes


def mxq(x, axis, fmt="e4m3"):
    dtype, down = {"e4m3": (ml_dtypes.float8_e4m3fn, 7), "e5m2": (ml_dtypes.float8_e5m2, 14)}[fmt]
    v = np.moveaxis(np.asarray(x, np.float32).astype(ml_dtypes.bfloat16).astype(np.float64), axis, -1)
    blocks = v.reshape(v.shape[:-1] + (-1, 32))
    amax = np.abs(blocks).max(-1, keepdims=True)
    byte = np.maximum(np.where(amax > 0, np.frexp(amax)[1] - 1 + 127, 0) - down, 1)
    scale = np.exp2(byte - 127.0)
    codes = (blocks / scale).astype(np.float32).astype(dtype).astype(np.float64)
    return np.moveaxis((codes * scale).reshape(v.shape), -1, axis)


WIDE = False


def mx_kscale(k):
    if not WIDE:
        return np.ones(k)
    levels = np.array([10, -10, 5, -5, 0])
    if k % 512:
        return np.exp2(np.random.permutation(np.resize(levels, k // 32))).repeat(32)
    a = np.empty((k // 512, 16))
    for p in range(k // 512):
        a[p, :8] = np.random.permutation(np.resize(levels, 8))
        for g in range(8):
            far = levels[np.abs(levels - a[p, g]) >= 10]
            a[p, g + 8] = far[np.random.randint(len(far))]
    return np.exp2(a.ravel()).repeat(32)


def f64(x):
    return np.asarray(x).astype(np.float64)


def striped(idx):
    return np.tile(idx.reshape(-1, 16).T, (8, 1)).astype(np.uint16)


def unstriped(offs):
    return offs[:16].T.reshape(-1).astype(np.int64)


E2M1 = np.array([0.0, 0.5, 1.0, 1.5, 2.0, 3.0, 4.0, 6.0, -0.0, -0.5, -1.0, -1.5, -2.0, -3.0, -4.0, -6.0])


def pack_weight(w, fmt):
    k, n = w.shape
    w = f64(np.asarray(w, np.float32).astype(ml_dtypes.bfloat16)).reshape(k // 32, 32, n)
    amax = np.abs(w).max(1)
    if fmt == "e4m3":
        byte = np.frexp(amax)[1] - 1 + 127 - 7
    else:
        mant, ex = np.frexp(amax / 6.0)
        byte = np.where(mant > 0.5, ex, ex - 1) + 127
    byte = np.clip(np.where(amax > 0, byte, 1), 1, 254)
    scaled = (w * np.exp2(127.0 - byte)[:, None, :]).reshape(k, n).astype(np.float32)
    by_word = np.ascontiguousarray(scaled.reshape(k // 512, 128, 4, n).transpose(0, 1, 3, 2))
    if fmt == "e4m3":
        words = by_word.astype(ml_dtypes.float8_e4m3fn).view(np.uint8)
    else:
        c = by_word.astype(ml_dtypes.float4_e2m1fn).view(np.uint8) & 0xF
        words = (c[..., 0::2] | (c[..., 1::2] << 4)).reshape(k // 512, 128, 2 * n)
    return np.ascontiguousarray(words), np.ascontiguousarray(byte.astype(np.uint8).reshape(k // 512, 16, n))


def unpack_weight(words, scales, fmt):
    g, _, n = scales.shape
    words = np.ascontiguousarray(words).reshape(g, 128, n, -1)
    if fmt == "e4m3":
        vals = words.view(ml_dtypes.float8_e4m3fn).astype(np.float64)
    else:
        nib = np.empty((g, 128, n, 4), np.uint8)
        nib[..., 0::2] = words & 0xF
        nib[..., 1::2] = words >> 4
        vals = E2M1[nib]
    vals = vals * np.repeat(np.exp2(scales.astype(np.float64) - 127.0), 8, axis=1)[..., None]
    return vals.transpose(0, 1, 3, 2).reshape(g * 512, n)


def gelu(v):
    return 0.5 * v * (1.0 + np.tanh(np.sqrt(2.0 / np.pi) * (v + 0.044715 * v**3)))


K, H, T, S, T2, P = 1536, 1024, 4096, 1024, 2048, 512

def setup_inputs():
    n = np.random.standard_normal
    s = mx_kscale(K)[:, None]
    u = mx_kscale(H)[:, None]
    w = mx_kscale(P)[:, None]
    tab_words, tab_scales = pack_weight(n((K, T)) * s, "e4m3")
    wl_words, wl_scales = pack_weight(n((H, H)) / np.sqrt(H) / u, "e2m1")
    return {
        "tab_words": tab_words, "tab_scales": tab_scales,
        "offs": striped(np.random.permutation(T)[:S]),
        "offs2": striped(np.random.permutation(T2)[:S]),
        "offs3": striped(np.random.permutation(T2)[:P]),
        "w1": (n((K, H)) / np.sqrt(K) / s).astype(np.float32),
        "wgs": np.exp(0.3 * n((128, S))).astype(np.float32),
        "page0": n((H, T2)).astype(np.float32),
        "gain": (np.exp(0.3 * n(H)) * u[:, 0]).astype(np.float32),
        "seedw": (np.exp(0.3 * n(P)) * w[:, 0]).astype(np.float32),
        "wl_words": wl_words, "wl_scales": wl_scales,
        "mix": (n((P, P)) / np.sqrt(P) / w).astype(np.float32),
    }

def reference(tab_words, tab_scales, offs, offs2, offs3, w1, wgs, page0, gain, seedw, wl_words, wl_scales, mix):
    v = unpack_weight(tab_words, tab_scales, "e4m3")[:, unstriped(offs)]
    h = mxq(f64(w1), 0, "e4m3").T @ v
    page = f64(page0).copy()
    page[:, unstriped(offs2)] = np.tile(f64(wgs), (H // 128, 1)) * h
    x = page[:, unstriped(offs3)]
    act = np.tanh(x)
    zl = act * f64(gain)[:, None]
    zr = (act * f64(seedw)[None, :]).T
    wl = unpack_weight(wl_words, wl_scales, "e2m1")
    return wl.T @ mxq(zl, 0, "e4m3") + mxq(zr, 0, "e4m3").T @ mxq(f64(mix), 0, "e4m3")

@@ -1,0 +1,374 @@
+from contextlib import ExitStack
+
+import concourse.mybir as mybir
+from concourse.masks import make_identity
+
+F32 = mybir.dt.float32
+BF16 = mybir.dt.bfloat16
+I32 = mybir.dt.int32
+U32 = mybir.dt.uint32
+U16 = mybir.dt.uint16
+U8 = mybir.dt.uint8
+FP8X4 = mybir.dt.float8_e4m3fn_x4
+FP4X4 = mybir.dt.float4_e2m1fn_x4
+MULT = mybir.AluOpType.mult
+COPY = mybir.ActivationFunctionType.Copy
+TANH = mybir.ActivationFunctionType.Tanh
+
+K, H, T, S, T2, SEEDS = 1536, 1024, 4096, 1024, 2048, 512
+P = 128
+PACK = 4
+K_PASS = P * PACK
+K_PASSES = K // K_PASS
+BANK = 512
+FLOPS = 2 * K * H * S + 2 * H * H * SEEDS + 2 * SEEDS * H * SEEDS
+
+
+def tile_list_tract_seed_filter_kernel(tc, tab_words, tab_scales, offs, offs2, offs3, w1, wgs, page0, gain, seedw, wl_words, wl_scales, mix, out):
+    nc = tc.nc
+    with ExitStack() as ctx:
+        lists = ctx.enter_context(tc.tile_pool(name="lists", bufs=1))
+        keep = ctx.enter_context(tc.tile_pool(name="keep", bufs=1))
+        psum = ctx.enter_context(tc.psum_pool(name="psum", bufs=1))
+
+        def sb(shape, dtype, name, tag=None):
+            return keep.tile(shape, dtype, name=name, tag=tag or name, align_bytes=64)
+
+        def bank(number, shape, dtype, name):
+            return psum.tile(shape, dtype, name=name, tag="bank%d" % number)
+
+        idx = lists.tile([P, S // 16], U16, name="idx")
+        idx2 = lists.tile([P, S // 16], U16, name="idx2")
+        idx3 = lists.tile([P, SEEDS // 16], U16, name="idx3")
+
+        def load_rows4(dst, src, a, cols):
+            nc.sync.dma_start(dst, src[a * K_PASS : (a + 1) * K_PASS, cols].rearrange("(p j) c -> p j c", j=PACK))
+
+        def interleave(dst, src):
+            nc.scalar.copy(dst.rearrange("p (c i) j -> p c j i", i=4), src.rearrange("p j (c i) -> p c j i", i=4))
+
+        def quantize(codes, scales, grouped):
+            nc.vector.quantize_mx(out=codes.bitcast(FP8X4), scales=scales, in_=grouped)
+
+        tab_sc = sb([P, T], U8, "tab_sc")
+        nc.vector.memset(tab_sc[:].bitcast(I32), 0)
+        for q in range(4):
+            nc.gpsimd.dma_start(tab_sc[32 * q : 32 * q + 4 * K_PASSES, :].bitcast(I32), tab_scales[:, 4 * q : 4 * q + 4, :].bitcast(I32))
+        warm = sb([P, 16], F32, "warm")
+        nc.gpsimd.memset(warm[:], 0.0)
+        nc.scalar.activation(warm[:, 8:9], warm[:, 0:1], TANH)
+        wl_sc = sb([P, 2, H], U8, "wl_sc")
+        nc.gpsimd.memset(wl_sc[:].bitcast(I32), 0)
+        ident32 = sb([P, P], F32, "ident32")
+        make_identity(nc, ident32[:])
+        ident16 = sb([P, P], BF16, "ident16")
+        make_identity(nc, ident16[:])
+
+        tab = [sb([P, T], I32, "tab%d" % a, "big%d" % a) for a in range(K_PASSES)]
+
+        def load_tab(a):
+            nc.sync.dma_start(tab[a][:], tab_words[a].rearrange("p t i -> p (t i)").bitcast(I32))
+
+        chunks = [(0, 128), (128, 128), (256, 256)]
+        raw = [[sb([P, PACK, width], F32, "raw%d_%d" % (n, a)) for a in range(K_PASSES)] for n, (first, width) in enumerate(chunks)]
+
+        def load_chunk(n):
+            first, width = chunks[n]
+            for a in range(K_PASSES):
+                load_rows4(raw[n][a][:], w1, a, slice(first, first + width))
+
+        pages = {}
+
+        def load_page(c):
+            pages[c] = sb([P, T2], F32, "page%d" % c, "page%d" % (c % 4))
+            if c < 4:
+                src = page0[c * P : (c + 1) * P, :]
+            else:
+                src = page0[K_PASS:, :].rearrange("(p t) c -> p t c", t=PACK)[:, c - 4, :]
+            nc.sync.dma_start(pages[c][:], src)
+
+        nc.sync.dma_start(idx[:], offs)
+        load_tab(0)
+        load_chunk(0)
+        load_tab(1)
+        load_tab(2)
+        nc.sync.dma_start(idx2[:], offs2)
+        wgs_nat = sb([P, S], F32, "wgs_nat")
+        nc.sync.dma_start(wgs_nat[:], wgs)
+        load_page(0)
+        load_chunk(1)
+        load_chunk(2)
+        nc.sync.dma_start(idx3[:], offs3)
+        load_page(1)
+        gain_nat = sb([P, 4], F32, "gain_nat")
+        with nc.allow_non_contiguous_dma(reason="one gain a partition"):
+            nc.sync.dma_start(gain_nat[:], gain[0:K_PASS].rearrange("(c p) -> p c", p=P))
+        gain_mx = sb([P, PACK], F32, "gain_mx")
+        nc.sync.dma_start(gain_mx[:], gain[K_PASS:].rearrange("(p t) -> p t", t=PACK))
+        seed_mx = sb([P, PACK], F32, "seed_mx")
+        nc.sync.dma_start(seed_mx[:], seedw.rearrange("(p t) -> p t", t=PACK))
+
+        v_sc = sb([P, S], U8, "v_sc")
+        nc.vector.tensor_copy(v_sc[:], tab_sc[:].indirect(idx[:]))
+        v_words = [sb([P, S], U32, "v_words%d" % a, "tab_sc" if a == 1 else None) for a in range(K_PASSES)]
+        for a in range(K_PASSES - 1):
+            nc.vector.tensor_copy(v_words[a][:], tab[a][:].bitcast(U32).indirect(idx[:]))
+
+        w_sc = [sb([P, K_PASSES, width], U8, "w_sc%d" % n) for n, (first, width) in enumerate(chunks)]
+        w_codes = {}
+
+        def quantize_chunk(n, codes, grouped_tag):
+            first, width = chunks[n]
+            w_codes[n] = codes
+            grouped = sb([P, K_PASSES, width, PACK], BF16, "grp%d" % n, grouped_tag)
+            for a in range(K_PASSES):
+                interleave(grouped[:, a], raw[n][a][:])
+                quantize(codes[:, a, :], w_sc[n][:, a, :], grouped[:, a].rearrange("p c j -> p (c j)"))
+
+        first_codes = sb([P, K_PASSES, P], U32, "first_codes")
+        quantize_chunk(0, first_codes[:], None)
+        last = K_PASSES - 1
+        for u in range(2):
+            nc.vector.tensor_copy(v_words[last][:, u * BANK : (u + 1) * BANK], tab[last][:].bitcast(U32).indirect(idx[:, 32 * u : 32 * (u + 1)]))
+
+        h_slot = [0, 1, 2, 3, 0, 1, 4, 5]
+        h_banks = [(0, 1), (2, 3), (0, 1), (2, 3), (0, 1), (2, 7), (0, 1), (2, 3)]
+        h = {}
+
+        def make_h(c, codes, scales):
+            h[c] = sb([P, S], F32, "h%d" % c, "slot%d" % h_slot[c])
+            for u in range(2):
+                cols = slice(u * BANK, (u + 1) * BANK)
+                acc = bank(h_banks[c][u], [P, BANK], F32, "h_acc%d_%d" % (c, u))
+                for a in range(K_PASSES):
+                    nc.tensor.matmul_mx(
+                        out=acc[:],
+                        lhsT=codes(a).bitcast(FP8X4),
+                        lhsT_scale=scales(a),
+                        rhs=v_words[a][:, cols].bitcast(FP8X4),
+                        rhs_scale=v_sc[4 * a :, cols],
+                        start=(a == 0),
+                        stop=(a == last),
+                    )
+                nc.scalar.copy(h[c][:, cols], acc[:])
+
+        def make_h_nat(c):
+            n = min(c, 2)
+            first = c * P - chunks[n][0]
+            make_h(c, lambda a: w_codes[n][:, a, first : first + P], lambda a: w_sc[n][:, a, first : first + P])
+
+        def scatter(c, weights, pieces):
+            width = S // pieces
+            for u in range(pieces):
+                cols = slice(u * width, (u + 1) * width)
+                nc.vector.tensor_tensor(pages[c][:].indirect(idx2[:, u * width // 16 : (u + 1) * width // 16]), h[c][:, cols], weights[:, cols], MULT)
+
+        act = {}
+        x_tag = ["w_sc0"] + ["x%d" % (c % 2) for c in range(1, 8)]
+        act_tag = ["raw0_0", "raw0_1", "raw0_2", "raw1_0", "raw1_1", "raw1_2", "raw1_1", "raw1_2"]
+
+        def fetch(c):
+            x = sb([P, SEEDS], F32, "x%d" % c, x_tag[c])
+            nc.vector.tensor_copy(x[:], pages[c][:].indirect(idx3[:]))
+            act[c] = sb([P, SEEDS], F32, "act%d" % c, act_tag[c])
+            nc.scalar.activation(act[c][:], x[:], TANH)
+
+        zl_t = sb([P, 4, K_PASS], BF16, "zl_t")
+
+        def turn_zl(c):
+            scaled = sb([P, SEEDS], BF16, "scaled%d" % c, "scaled%d" % (c % 2))
+            nc.scalar.activation(scaled[:], act[c][:], COPY, scale=gain_nat[:, c : c + 1])
+            turned = bank(4, [P, 4, P], BF16, "turned%d" % c)
+            for m in range(4):
+                nc.tensor.transpose(turned[:, m, :], scaled[:, m * P : (m + 1) * P], ident16[:])
+            nc.scalar.copy(zl_t[:, :, c * P : (c + 1) * P], turned[:])
+
+        make_h_nat(0)
+        scatter(0, wgs_nat, 1)
+        later_codes = sb([P, K_PASSES * 3 * P], U32, "later_codes", "slot0")
+        quantize_chunk(1, later_codes[:, : K_PASSES * P].rearrange("p (a c) -> p a c", a=K_PASSES), "first_codes")
+        quantize_chunk(2, later_codes[:, K_PASSES * P :].rearrange("p (a c) -> p a c", a=K_PASSES), "w_sc0")
+        make_h_nat(1)
+        fetch(0)
+        make_h_nat(2)
+        make_h_nat(3)
+        turn_zl(0)
+
+        raw_a = sb([P, 2, PACK, K_PASS], F32, "raw_a", "big0")
+        raw_b = sb([P, 2, PACK, K_PASS], F32, "raw_b", "big1")
+        raw_hi = [raw_a[:, 0], raw_a[:, 1], raw_b[:, 0]]
+        hi_cols = slice(K_PASS, H)
+        load_rows4(raw_hi[0], w1, 0, hi_cols)
+        load_rows4(raw_hi[1], w1, 1, hi_cols)
+        load_page(2)
+        load_rows4(raw_hi[2], w1, 2, hi_cols)
+        load_page(3)
+        load_rows4(raw_b[:, 1], mix, 0, slice(0, SEEDS))
+        wgs_mx = sb([P, PACK, S], F32, "wgs_mx", "big2")
+        for g in range(4):
+            nc.sync.dma_start(wgs_mx[32 * g : 32 * (g + 1), :, :], wgs.rearrange("(q t) j -> q t j", t=PACK))
+
+        scatter(1, wgs_nat, 2)
+        fetch(1)
+        turn_zl(1)
+
+        hi_grouped = {}
+
+        def group_hi(a):
+            hi_grouped[a] = sb([P, PACK, P, PACK], BF16, "hi_grp%d" % a, "hi_grp%d" % (a % 2))
+            nc.scalar.copy(hi_grouped[a][:].rearrange("p t m j -> p m j t"), raw_hi[a].rearrange("p j (m t) -> p m j t", t=PACK))
+
+        hi_sc = sb([P, K_PASSES, K_PASS], U8, "hi_sc")
+        group_hi(0)
+        group_hi(1)
+        scatter(2, wgs_nat, 1)
+        hi_codes01 = sb([P, 2, K_PASS], U32, "hi_codes01", "slot2")
+        for a in range(2):
+            quantize(hi_codes01[:, a, :], hi_sc[:, a, :], hi_grouped[a][:].rearrange("p t m j -> p (t m j)"))
+        fetch(2)
+        group_hi(2)
+        turn_zl(2)
+        scatter(3, wgs_nat, 1)
+        hi_codes2 = sb([P, K_PASS], U32, "hi_codes2", "slot3")
+        quantize(hi_codes2[:], hi_sc[:, 2, :], hi_grouped[2][:].rearrange("p t m j -> p (t m j)"))
+        hi_codes = [hi_codes01[:, 0, :], hi_codes01[:, 1, :], hi_codes2[:]]
+
+        def make_h_mx(c):
+            t = c - 4
+            make_h(c, lambda a: hi_codes[a][:, t * P : (t + 1) * P], lambda a: hi_sc[:, a, t * P : (t + 1) * P])
+
+        load_page(4)
+        wl_w = sb([P, 2, 2 * H], U8, "wl_w")
+        nc.sync.dma_start(wl_w[:].bitcast(I32), wl_words.rearrange("a p c -> p a c").bitcast(I32))
+        for q in range(4):
+            nc.sync.dma_start(wl_sc[32 * q : 32 * q + 4, :, :].bitcast(I32), wl_scales[:, 4 * q : 4 * q + 4, :].rearrange("a r c -> r a c").bitcast(I32))
+        load_page(5)
+        load_page(6)
+        load_page(7)
+
+        make_h_mx(4)
+        fetch(3)
+        make_h_mx(5)
+        turn_zl(3)
+        zl0 = sb([P, SEEDS, PACK], BF16, "zl0", "raw2_0")
+        zl0_words = zl0[:].rearrange("p m j -> p (m j)").bitcast(F32)
+        for half in range(2):
+            back = bank(5 + half, [P, 2, 2, P], F32, "back%d" % half)
+            for m in range(2):
+                words = zl_t[:, 2 * half + m, :].bitcast(F32)
+                for u in range(2):
+                    nc.tensor.transpose(back[:, m, u, :], words[:, u : 2 * P : 2], ident32[:])
+            nc.scalar.copy(
+                zl0_words[:, half * BANK : (half + 1) * BANK].rearrange("p (a m u) -> p a m u", a=2, u=2),
+                back[:].rearrange("p a u m -> p a m u"),
+            )
+        mix_grouped = sb([P, SEEDS, PACK], BF16, "mix_grp", "hi_grp1")
+        interleave(mix_grouped[:], raw_b[:, 1])
+        make_h_mx(6)
+        make_h_mx(7)
+
+        zr0_planes = sb([P, PACK, K_PASS], BF16, "zr0_planes", "raw2_2")
+        for i in range(PACK):
+            turned = bank(7, [P, 4, P], F32, "zr0_turned%d" % i)
+            for c in range(4):
+                nc.tensor.transpose(turned[:, c, :], act[c][:, i:SEEDS:PACK], ident32[:])
+            nc.scalar.activation(zr0_planes[:, i, :], turned[:].rearrange("p c r -> p (c r)"), COPY, scale=seed_mx[:, i : i + 1])
+        zr0 = sb([P, K_PASS, PACK], BF16, "zr0", "raw2_1")
+        interleave(zr0[:], zr0_planes[:])
+
+        zl1 = sb([P, SEEDS, PACK], BF16, "zl1")
+        zr1 = sb([P, K_PASS, PACK], BF16, "zr1")
+
+        def finish_zr(c):
+            t = c - 4
+            turned = bank(7, [P, PACK, P], F32, "zr1_turned%d" % t)
+            planes = sb([P, PACK, P], BF16, "zr1_planes%d" % t, "scaled%d" % (t % 2))
+            for i in range(PACK):
+                nc.tensor.transpose(turned[:, i, :], act[c][:, i:SEEDS:PACK], ident32[:])
+            for i in range(PACK):
+                nc.scalar.activation(planes[:, i, :], turned[:, i, :], COPY, scale=seed_mx[:, i : i + 1])
+            nc.scalar.copy(zr1[:].rearrange("q (p t) i -> q t p i", t=PACK)[:, t], planes[:].rearrange("q i p -> q p i"))
+
+        def finish_zl(c):
+            t = c - 4
+            nc.scalar.activation(zl1[:, :, t], act[c][:], COPY, scale=gain_mx[:, t : t + 1])
+
+        acc_out = {}
+
+        def left_pass(n, a, codes, scales, start, stop):
+            nc.tensor.matmul_mx(
+                out=acc_out[n][:],
+                lhsT=wl_w[:, a, 2 * n * P : 2 * (n + 1) * P].bitcast(FP4X4),
+                lhsT_scale=wl_sc[:, a, n * P : (n + 1) * P],
+                rhs=codes.bitcast(FP8X4),
+                rhs_scale=scales,
+                start=start,
+                stop=stop,
+            )
+
+        def right_pass(n, codes, scales, stop):
+            cols = slice((n % 4) * P, (n % 4 + 1) * P)
+            nc.tensor.matmul_mx(
+                out=acc_out[n][:],
+                lhsT=codes[:, cols].bitcast(FP8X4),
+                lhsT_scale=scales[:, cols],
+                rhs=early_codes[:, 1, :].bitcast(FP8X4),
+                rhs_scale=early_sc[:, 1, :],
+                start=False,
+                stop=stop,
+            )
+
+        scatter(4, wgs_mx[:, 0, :], 2)
+        fetch(4)
+        finish_zl(4)
+        finish_zr(4)
+        scatter(5, wgs_mx[:, 1, :], 1)
+        early_codes = sb([P, 2, SEEDS], U32, "early_codes", "slot1")
+        early_sc = sb([P, 2, SEEDS], U8, "early_sc")
+        quantize(early_codes[:, 0, :], early_sc[:, 0, :], zl0[:].rearrange("p m j -> p (m j)"))
+        quantize(early_codes[:, 1, :], early_sc[:, 1, :], mix_grouped[:].rearrange("p m j -> p (m j)"))
+        fetch(5)
+        finish_zl(5)
+        finish_zr(5)
+        for n in range(7):
+            acc_out[n] = bank(n, [P, SEEDS], F32, "acc_out%d" % n)
+            left_pass(n, 0, early_codes[:, 0, :], early_sc[:, 0, :], True, False)
+        scatter(6, wgs_mx[:, 2, :], 1)
+        fetch(6)
+        finish_zl(6)
+        finish_zr(6)
+        scatter(7, wgs_mx[:, 3, :], 1)
+        zr0_codes = sb([P, K_PASS], U32, "zr0_codes", "slot5")
+        zr0_sc = sb([P, K_PASS], U8, "zr0_sc")
+        quantize(zr0_codes[:], zr0_sc[:], zr0[:].rearrange("p n i -> p (n i)"))
+        fetch(7)
+        for n in range(4):
+            right_pass(n, zr0_codes, zr0_sc, False)
+        nc.vector.tensor_scalar(zl1[:, :, 3], act[7][:], gain_mx[:, 3:4], None, MULT)
+        zl1_codes = sb([P, SEEDS], U32, "zl1_codes")
+        zl1_sc = sb([P, SEEDS], U8, "zl1_sc")
+        quantize(zl1_codes[:], zl1_sc[:], zl1[:].rearrange("p m j -> p (m j)"))
+        finish_zr(7)
+        zr1_codes = sb([P, K_PASS], U32, "zr1_codes")
+        zr1_sc = sb([P, K_PASS], U8, "zr1_sc")
+        quantize(zr1_codes[:], zr1_sc[:], zr1[:].rearrange("p n i -> p (n i)"))
+
+        staged = sb([P, 8, SEEDS], F32, "staged", "big0")
+
+        def hand_out(n):
+            if n % 2 == 0:
+                nc.scalar.copy(staged[:, n, :], acc_out[n][:])
+            else:
+                nc.vector.tensor_copy(staged[:, n, :], acc_out[n][:])
+            nc.sync.dma_start(out[n * P : (n + 1) * P, :], staged[:, n, :])
+
+        for n in range(7):
+            left_pass(n, 1, zl1_codes[:], zl1_sc[:], False, n < 4)
+            if n < 4:
+                hand_out(n)
+        acc_out[7] = bank(7, [P, SEEDS], F32, "acc_out7")
+        left_pass(7, 0, early_codes[:, 0, :], early_sc[:, 0, :], True, False)
+        left_pass(7, 1, zl1_codes[:], zl1_sc[:], False, False)
+        for n in range(4, 8):
+            right_pass(n, zr1_codes, zr1_sc, True)
+            hand_out(n)

@@ -52,8 +52,6 @@ def tile_list_tract_seed_filter_kernel(tc, tab_words, tab_scales, offs, offs2, o
 
         tab_sc = sb([P, T], U8, "tab_sc")
         nc.vector.memset(tab_sc[:].bitcast(I32), 0)
-        for q in range(4):
-            nc.gpsimd.dma_start(tab_sc[32 * q : 32 * q + 4 * K_PASSES, :].bitcast(I32), tab_scales[:, 4 * q : 4 * q + 4, :].bitcast(I32))
         warm = sb([P, 16], F32, "warm")
         nc.gpsimd.memset(warm[:], 0.0)
         nc.scalar.activation(warm[:, 8:9], warm[:, 0:1], TANH)
@@ -70,7 +68,7 @@ def tile_list_tract_seed_filter_kernel(tc, tab_words, tab_scales, offs, offs2, o
             nc.sync.dma_start(tab[a][:], tab_words[a].rearrange("p t i -> p (t i)").bitcast(I32))
 
         chunks = [(0, 128), (128, 128), (256, 256)]
-        raw = [[sb([P, PACK, width], F32, "raw%d_%d" % (n, a)) for a in range(K_PASSES)] for n, (first, width) in enumerate(chunks)]
+        raw = [[sb([P, PACK, width], F32, "raw%d_%d" % (n, a), "slot1" if (n, a) == (2, 2) else None) for a in range(K_PASSES)] for n, (first, width) in enumerate(chunks)]
 
         def load_chunk(n):
             first, width = chunks[n]
@@ -89,13 +87,16 @@ def tile_list_tract_seed_filter_kernel(tc, tab_words, tab_scales, offs, offs2, o
 
         nc.sync.dma_start(idx[:], offs)
         load_tab(0)
-        load_chunk(0)
+        for q in range(4):
+            nc.sync.dma_start(tab_sc[32 * q : 32 * q + 4 * K_PASSES, :].bitcast(I32), tab_scales[:, 4 * q : 4 * q + 4, :].bitcast(I32))
         load_tab(1)
+        load_chunk(0)
         load_tab(2)
         nc.sync.dma_start(idx2[:], offs2)
         wgs_nat = sb([P, S], F32, "wgs_nat")
-        nc.sync.dma_start(wgs_nat[:], wgs)
+        nc.sync.dma_start(wgs_nat[:, :BANK], wgs[:, :BANK])
         load_page(0)
+        nc.sync.dma_start(wgs_nat[:, BANK:], wgs[:, BANK:])
         load_chunk(1)
         load_chunk(2)
         nc.sync.dma_start(idx3[:], offs3)
@@ -109,10 +110,10 @@ def tile_list_tract_seed_filter_kernel(tc, tab_words, tab_scales, offs, offs2, o
         nc.sync.dma_start(seed_mx[:], seedw.rearrange("(p t) -> p t", t=PACK))
 
         v_sc = sb([P, S], U8, "v_sc")
+        v_words = [sb([P, S], U32, "v_words%d" % a) for a in range(K_PASSES)]
+        nc.vector.tensor_copy(v_words[0][:], tab[0][:].bitcast(U32).indirect(idx[:]))
         nc.vector.tensor_copy(v_sc[:], tab_sc[:].indirect(idx[:]))
-        v_words = [sb([P, S], U32, "v_words%d" % a, "tab_sc" if a == 1 else None) for a in range(K_PASSES)]
-        for a in range(K_PASSES - 1):
-            nc.vector.tensor_copy(v_words[a][:], tab[a][:].bitcast(U32).indirect(idx[:]))
+        nc.vector.tensor_copy(v_words[1][:], tab[1][:].bitcast(U32).indirect(idx[:]))
 
         w_sc = [sb([P, K_PASSES, width], U8, "w_sc%d" % n) for n, (first, width) in enumerate(chunks)]
         w_codes = {}
@@ -132,7 +133,7 @@ def tile_list_tract_seed_filter_kernel(tc, tab_words, tab_scales, offs, offs2, o
             nc.vector.tensor_copy(v_words[last][:, u * BANK : (u + 1) * BANK], tab[last][:].bitcast(U32).indirect(idx[:, 32 * u : 32 * (u + 1)]))
 
         h_slot = [0, 1, 2, 3, 0, 1, 4, 5]
-        h_banks = [(0, 1), (2, 3), (0, 1), (2, 3), (0, 1), (2, 7), (0, 1), (2, 3)]
+        h_banks = [(0, 1), (2, 3), (0, 1), (2, 4), (0, 1), (2, 7), (5, 6), (0, 3)]
         h = {}
 
         def make_h(c, codes, scales):
@@ -164,14 +165,17 @@ def tile_list_tract_seed_filter_kernel(tc, tab_words, tab_scales, offs, offs2, o
                 nc.vector.tensor_tensor(pages[c][:].indirect(idx2[:, u * width // 16 : (u + 1) * width // 16]), h[c][:, cols], weights[:, cols], MULT)
 
         act = {}
-        x_tag = ["w_sc0"] + ["x%d" % (c % 2) for c in range(1, 8)]
-        act_tag = ["raw0_0", "raw0_1", "raw0_2", "raw1_0", "raw1_1", "raw1_2", "raw1_1", "raw1_2"]
+        x_tag = ["w_sc0", "slot0", "x0", "x1", "x0", "x1", "x0", "x1"]
+        act_tag = ["raw0_0", "big0", "raw0_2", "raw1_0", "raw1_1", "raw1_2", "raw1_1", "raw1_2"]
 
-        def fetch(c):
+        def fetch(c, pieces=1):
             x = sb([P, SEEDS], F32, "x%d" % c, x_tag[c])
-            nc.vector.tensor_copy(x[:], pages[c][:].indirect(idx3[:]))
             act[c] = sb([P, SEEDS], F32, "act%d" % c, act_tag[c])
-            nc.scalar.activation(act[c][:], x[:], TANH)
+            width = SEEDS // pieces
+            for u in range(pieces):
+                cols = slice(u * width, (u + 1) * width)
+                nc.vector.tensor_copy(x[:, cols], pages[c][:].indirect(idx3[:, u * width // 16 : (u + 1) * width // 16]))
+                nc.scalar.activation(act[c][:, cols], x[:, cols], TANH)
 
         zl_t = sb([P, 4, K_PASS], BF16, "zl_t")
 
@@ -184,7 +188,7 @@ def tile_list_tract_seed_filter_kernel(tc, tab_words, tab_scales, offs, offs2, o
             nc.scalar.copy(zl_t[:, :, c * P : (c + 1) * P], turned[:])
 
         make_h_nat(0)
-        scatter(0, wgs_nat, 1)
+        scatter(0, wgs_nat, 2)
         later_codes = sb([P, K_PASSES * 3 * P], U32, "later_codes", "slot0")
         quantize_chunk(1, later_codes[:, : K_PASSES * P].rearrange("p (a c) -> p a c", a=K_PASSES), "first_codes")
         quantize_chunk(2, later_codes[:, K_PASSES * P :].rearrange("p (a c) -> p a c", a=K_PASSES), "w_sc0")
@@ -194,48 +198,45 @@ def tile_list_tract_seed_filter_kernel(tc, tab_words, tab_scales, offs, offs2, o
         make_h_nat(3)
         turn_zl(0)
 
-        raw_a = sb([P, 2, PACK, K_PASS], F32, "raw_a", "big0")
+        raw_a = sb([P, PACK, K_PASS], F32, "raw_a", "big0")
         raw_b = sb([P, 2, PACK, K_PASS], F32, "raw_b", "big1")
-        raw_hi = [raw_a[:, 0], raw_a[:, 1], raw_b[:, 0]]
+        raw_mix = sb([P, PACK, SEEDS], F32, "raw_mix")
+        raw_hi = [raw_a[:], raw_b[:, 0], raw_b[:, 1]]
         hi_cols = slice(K_PASS, H)
         load_rows4(raw_hi[0], w1, 0, hi_cols)
         load_rows4(raw_hi[1], w1, 1, hi_cols)
-        load_page(2)
         load_rows4(raw_hi[2], w1, 2, hi_cols)
-        load_page(3)
-        load_rows4(raw_b[:, 1], mix, 0, slice(0, SEEDS))
+        load_page(2)
+        load_rows4(raw_mix[:], mix, 0, slice(0, SEEDS))
         wgs_mx = sb([P, PACK, S], F32, "wgs_mx", "big2")
         for g in range(4):
             nc.sync.dma_start(wgs_mx[32 * g : 32 * (g + 1), :, :], wgs.rearrange("(q t) j -> q t j", t=PACK))
-
-        scatter(1, wgs_nat, 2)
-        fetch(1)
-        turn_zl(1)
+        load_page(3)
 
         hi_grouped = {}
 
         def group_hi(a):
-            hi_grouped[a] = sb([P, PACK, P, PACK], BF16, "hi_grp%d" % a, "hi_grp%d" % (a % 2))
+            hi_grouped[a] = sb([P, PACK, P, PACK], BF16, "hi_grp%d" % a)
             nc.scalar.copy(hi_grouped[a][:].rearrange("p t m j -> p m j t"), raw_hi[a].rearrange("p j (m t) -> p m j t", t=PACK))
 
         hi_sc = sb([P, K_PASSES, K_PASS], U8, "hi_sc")
+        scatter(1, wgs_nat, 2)
         group_hi(0)
+        fetch(1)
         group_hi(1)
-        scatter(2, wgs_nat, 1)
-        hi_codes01 = sb([P, 2, K_PASS], U32, "hi_codes01", "slot2")
-        for a in range(2):
-            quantize(hi_codes01[:, a, :], hi_sc[:, a, :], hi_grouped[a][:].rearrange("p t m j -> p (t m j)"))
-        fetch(2)
         group_hi(2)
+        turn_zl(1)
+        scatter(2, wgs_nat, 1)
+        hi_codes = sb([P, K_PASSES, K_PASS], U32, "hi_codes", "slot2")
+        for a in range(K_PASSES):
+            quantize(hi_codes[:, a, :], hi_sc[:, a, :], hi_grouped[a][:].rearrange("p t m j -> p (t m j)"))
+        fetch(2)
         turn_zl(2)
         scatter(3, wgs_nat, 1)
-        hi_codes2 = sb([P, K_PASS], U32, "hi_codes2", "slot3")
-        quantize(hi_codes2[:], hi_sc[:, 2, :], hi_grouped[2][:].rearrange("p t m j -> p (t m j)"))
-        hi_codes = [hi_codes01[:, 0, :], hi_codes01[:, 1, :], hi_codes2[:]]
 
         def make_h_mx(c):
             t = c - 4
-            make_h(c, lambda a: hi_codes[a][:, t * P : (t + 1) * P], lambda a: hi_sc[:, a, t * P : (t + 1) * P])
+            make_h(c, lambda a: hi_codes[:, a, t * P : (t + 1) * P], lambda a: hi_sc[:, a, t * P : (t + 1) * P])
 
         load_page(4)
         wl_w = sb([P, 2, 2 * H], U8, "wl_w")
@@ -246,9 +247,9 @@ def tile_list_tract_seed_filter_kernel(tc, tab_words, tab_scales, offs, offs2, o
         load_page(6)
         load_page(7)
 
-        make_h_mx(4)
+        for c in range(4, 8):
+            make_h_mx(c)
         fetch(3)
-        make_h_mx(5)
         turn_zl(3)
         zl0 = sb([P, SEEDS, PACK], BF16, "zl0", "raw2_0")
         zl0_words = zl0[:].rearrange("p m j -> p (m j)").bitcast(F32)
@@ -263,11 +264,9 @@ def tile_list_tract_seed_filter_kernel(tc, tab_words, tab_scales, offs, offs2, o
                 back[:].rearrange("p a u m -> p a m u"),
             )
         mix_grouped = sb([P, SEEDS, PACK], BF16, "mix_grp", "hi_grp1")
-        interleave(mix_grouped[:], raw_b[:, 1])
-        make_h_mx(6)
-        make_h_mx(7)
+        interleave(mix_grouped[:], raw_mix[:])
 
-        zr0_planes = sb([P, PACK, K_PASS], BF16, "zr0_planes", "raw2_2")
+        zr0_planes = sb([P, PACK, K_PASS], BF16, "zr0_planes", "slot3")
         for i in range(PACK):
             turned = bank(7, [P, 4, P], F32, "zr0_turned%d" % i)
             for c in range(4):
@@ -318,7 +317,7 @@ def tile_list_tract_seed_filter_kernel(tc, tab_words, tab_scales, offs, offs2, o
                 stop=stop,
             )
 
-        scatter(4, wgs_mx[:, 0, :], 2)
+        scatter(4, wgs_mx[:, 0, :], 1)
         fetch(4)
         finish_zl(4)
         finish_zr(4)
@@ -341,10 +340,12 @@ def tile_list_tract_seed_filter_kernel(tc, tab_words, tab_scales, offs, offs2, o
         zr0_codes = sb([P, K_PASS], U32, "zr0_codes", "slot5")
         zr0_sc = sb([P, K_PASS], U8, "zr0_sc")
         quantize(zr0_codes[:], zr0_sc[:], zr0[:].rearrange("p n i -> p (n i)"))
-        fetch(7)
+        fetch(7, 2)
         for n in range(4):
             right_pass(n, zr0_codes, zr0_sc, False)
-        nc.vector.tensor_scalar(zl1[:, :, 3], act[7][:], gain_mx[:, 3:4], None, MULT)
+        for u in range(2):
+            cols = slice(u * SEEDS // 2, (u + 1) * SEEDS // 2)
+            nc.vector.tensor_scalar(zl1[:, cols, 3], act[7][:, cols], gain_mx[:, 3:4], None, MULT)
         zl1_codes = sb([P, SEEDS], U32, "zl1_codes")
         zl1_sc = sb([P, SEEDS], U8, "zl1_sc")
         quantize(zl1_codes[:], zl1_sc[:], zl1[:].rearrange("p m j -> p (m j)"))
@@ -356,7 +357,7 @@ def tile_list_tract_seed_filter_kernel(tc, tab_words, tab_scales, offs, offs2, o
         staged = sb([P, 8, SEEDS], F32, "staged", "big0")
 
         def hand_out(n):
-            if n % 2 == 0:
+            if n in (2, 3, 5, 7):
                 nc.scalar.copy(staged[:, n, :], acc_out[n][:])
             else:
                 nc.vector.tensor_copy(staged[:, n, :], acc_out[n][:])

@@ -20,7 +20,16 @@ P = 128
 PACK = 4
 K_PASS = P * PACK
 K_PASSES = K // K_PASS
+LAST_PASS = K_PASSES - 1
 BANK = 512
+LIST_ROWS = 16
+QUADRANTS = 4
+LOW_TILES = 4
+ROW_TILES = H // P
+LAST_TILE = ROW_TILES - 1
+PAGE_SLOTS = 4
+RUN = 4
+LOW_CHUNKS = [(0, P), (P, P), (2 * P, 2 * P)]
 FLOPS = 2 * K * H * S + 2 * H * H * SEEDS + 2 * SEEDS * H * SEEDS
 
 
@@ -37,24 +46,26 @@ def tile_list_tract_seed_filter_kernel(tc, tab_words, tab_scales, offs, offs2, o
         def bank(number, shape, dtype, name):
             return psum.tile(shape, dtype, name=name, tag="bank%d" % number)
 
-        idx = lists.tile([P, S // 16], U16, name="idx")
-        idx2 = lists.tile([P, S // 16], U16, name="idx2")
-        idx3 = lists.tile([P, SEEDS // 16], U16, name="idx3")
+        def entries(list_tile, first, count):
+            return list_tile[:, first // LIST_ROWS : (first + count) // LIST_ROWS]
 
-        def load_rows4(dst, src, a, cols):
-            nc.sync.dma_start(dst, src[a * K_PASS : (a + 1) * K_PASS, cols].rearrange("(p j) c -> p j c", j=PACK))
+        def load_pass_rows(dst, src, a, cols):
+            nc.sync.dma_start(dst, src[a * K_PASS : (a + 1) * K_PASS, cols].rearrange("(p i) c -> p i c", i=PACK))
 
-        def interleave(dst, src):
-            nc.scalar.copy(dst.rearrange("p (c i) j -> p c j i", i=4), src.rearrange("p j (c i) -> p c j i", i=4))
+        def interleave(grouped, planes):
+            nc.scalar.copy(grouped.rearrange("p (c n) i -> p c i n", n=RUN), planes.rearrange("p i (c n) -> p c i n", n=RUN))
 
         def quantize(codes, scales, grouped):
             nc.vector.quantize_mx(out=codes.bitcast(FP8X4), scales=scales, in_=grouped)
 
+        idx = lists.tile([P, S // LIST_ROWS], U16, name="idx")
+        idx2 = lists.tile([P, S // LIST_ROWS], U16, name="idx2")
+        idx3 = lists.tile([P, SEEDS // LIST_ROWS], U16, name="idx3")
+
         tab_sc = sb([P, T], U8, "tab_sc")
         nc.vector.memset(tab_sc[:].bitcast(I32), 0)
-        warm = sb([P, 16], F32, "warm")
-        nc.gpsimd.memset(warm[:], 0.0)
-        nc.scalar.activation(warm[:, 8:9], warm[:, 0:1], TANH)
+        for q in range(QUADRANTS):
+            nc.gpsimd.dma_start(tab_sc[32 * q : 32 * q + 4 * K_PASSES, :].bitcast(I32), tab_scales[:, 4 * q : 4 * q + 4, :].bitcast(I32))
         wl_sc = sb([P, 2, H], U8, "wl_sc")
         nc.gpsimd.memset(wl_sc[:].bitcast(I32), 0)
         ident32 = sb([P, P], F32, "ident32")
@@ -67,77 +78,81 @@ def tile_list_tract_seed_filter_kernel(tc, tab_words, tab_scales, offs, offs2, o
         def load_tab(a):
             nc.sync.dma_start(tab[a][:], tab_words[a].rearrange("p t i -> p (t i)").bitcast(I32))
 
-        chunks = [(0, 128), (128, 128), (256, 256)]
-        raw = [[sb([P, PACK, width], F32, "raw%d_%d" % (n, a), "slot1" if (n, a) == (2, 2) else None) for a in range(K_PASSES)] for n, (first, width) in enumerate(chunks)]
+        low_raw = [
+            [sb([P, PACK, width], F32, "raw%d_%d" % (n, a), "slot1" if (n, a) == (len(LOW_CHUNKS) - 1, LAST_PASS) else None) for a in range(K_PASSES)]
+            for n, (first, width) in enumerate(LOW_CHUNKS)
+        ]
 
-        def load_chunk(n):
-            first, width = chunks[n]
+        def load_low_chunk(n):
+            first, width = LOW_CHUNKS[n]
             for a in range(K_PASSES):
-                load_rows4(raw[n][a][:], w1, a, slice(first, first + width))
+                load_pass_rows(low_raw[n][a][:], w1, a, slice(first, first + width))
 
         pages = {}
 
         def load_page(c):
-            pages[c] = sb([P, T2], F32, "page%d" % c, "page%d" % (c % 4))
-            if c < 4:
-                src = page0[c * P : (c + 1) * P, :]
+            pages[c] = sb([P, T2], F32, "page%d" % c, "page%d" % (c % PAGE_SLOTS))
+            if c < LOW_TILES:
+                rows = page0[c * P : (c + 1) * P, :]
             else:
-                src = page0[K_PASS:, :].rearrange("(p t) c -> p t c", t=PACK)[:, c - 4, :]
-            nc.sync.dma_start(pages[c][:], src)
+                rows = page0[K_PASS:, :].rearrange("(p t) c -> p t c", t=PACK)[:, c - LOW_TILES, :]
+            nc.sync.dma_start(pages[c][:], rows)
 
         nc.sync.dma_start(idx[:], offs)
         load_tab(0)
-        for q in range(4):
-            nc.sync.dma_start(tab_sc[32 * q : 32 * q + 4 * K_PASSES, :].bitcast(I32), tab_scales[:, 4 * q : 4 * q + 4, :].bitcast(I32))
         load_tab(1)
-        load_chunk(0)
+        load_low_chunk(0)
         load_tab(2)
         nc.sync.dma_start(idx2[:], offs2)
-        wgs_nat = sb([P, S], F32, "wgs_nat")
-        nc.sync.dma_start(wgs_nat[:, :BANK], wgs[:, :BANK])
+        wgs_low = sb([P, S], F32, "wgs_low")
+        nc.sync.dma_start(wgs_low[:, :BANK], wgs[:, :BANK])
         load_page(0)
-        nc.sync.dma_start(wgs_nat[:, BANK:], wgs[:, BANK:])
-        load_chunk(1)
-        load_chunk(2)
+        nc.sync.dma_start(wgs_low[:, BANK:], wgs[:, BANK:])
+        load_low_chunk(1)
+        load_low_chunk(2)
         nc.sync.dma_start(idx3[:], offs3)
         load_page(1)
-        gain_nat = sb([P, 4], F32, "gain_nat")
-        with nc.allow_non_contiguous_dma(reason="one gain a partition"):
-            nc.sync.dma_start(gain_nat[:], gain[0:K_PASS].rearrange("(c p) -> p c", p=P))
-        gain_mx = sb([P, PACK], F32, "gain_mx")
-        nc.sync.dma_start(gain_mx[:], gain[K_PASS:].rearrange("(p t) -> p t", t=PACK))
-        seed_mx = sb([P, PACK], F32, "seed_mx")
-        nc.sync.dma_start(seed_mx[:], seedw.rearrange("(p t) -> p t", t=PACK))
+        gain_low = sb([P, LOW_TILES], F32, "gain_low")
+        with nc.allow_non_contiguous_dma(reason="one gain for each partition and low tile"):
+            nc.sync.dma_start(gain_low[:], gain[0:K_PASS].rearrange("(c p) -> p c", p=P))
+        gain_high = sb([P, PACK], F32, "gain_high")
+        nc.sync.dma_start(gain_high[:], gain[K_PASS:].rearrange("(p t) -> p t", t=PACK))
+        seed_w = sb([P, PACK], F32, "seed_w")
+        nc.sync.dma_start(seed_w[:], seedw.rearrange("(q i) -> q i", i=PACK))
 
         v_sc = sb([P, S], U8, "v_sc")
-        v_words = [sb([P, S], U32, "v_words%d" % a) for a in range(K_PASSES)]
+        v_words = [sb([P, S], U32, "v_words%d" % a) for a in range(LAST_PASS)]
         nc.vector.tensor_copy(v_words[0][:], tab[0][:].bitcast(U32).indirect(idx[:]))
         nc.vector.tensor_copy(v_sc[:], tab_sc[:].indirect(idx[:]))
         nc.vector.tensor_copy(v_words[1][:], tab[1][:].bitcast(U32).indirect(idx[:]))
 
-        w_sc = [sb([P, K_PASSES, width], U8, "w_sc%d" % n) for n, (first, width) in enumerate(chunks)]
-        w_codes = {}
+        low_sc = [sb([P, K_PASSES, width], U8, "low_sc%d" % n) for n, (first, width) in enumerate(LOW_CHUNKS)]
+        low_codes = {}
 
-        def quantize_chunk(n, codes, grouped_tag):
-            first, width = chunks[n]
-            w_codes[n] = codes
-            grouped = sb([P, K_PASSES, width, PACK], BF16, "grp%d" % n, grouped_tag)
+        def quantize_low_chunk(n, codes, grouped_tag):
+            first, width = LOW_CHUNKS[n]
+            low_codes[n] = codes
+            grouped = sb([P, K_PASSES, width, PACK], BF16, "low_grouped%d" % n, grouped_tag)
             for a in range(K_PASSES):
-                interleave(grouped[:, a], raw[n][a][:])
-                quantize(codes[:, a, :], w_sc[n][:, a, :], grouped[:, a].rearrange("p c j -> p (c j)"))
+                interleave(grouped[:, a], low_raw[n][a][:])
+                quantize(codes[:, a, :], low_sc[n][:, a, :], grouped[:, a].rearrange("p c i -> p (c i)"))
 
         first_codes = sb([P, K_PASSES, P], U32, "first_codes")
-        quantize_chunk(0, first_codes[:], None)
-        last = K_PASSES - 1
+        quantize_low_chunk(0, first_codes[:], "tab_sc")
+        v_words.append(sb([P, S], U32, "v_words%d" % LAST_PASS, "tab_sc"))
         for u in range(2):
-            nc.vector.tensor_copy(v_words[last][:, u * BANK : (u + 1) * BANK], tab[last][:].bitcast(U32).indirect(idx[:, 32 * u : 32 * (u + 1)]))
+            nc.vector.tensor_copy(v_words[LAST_PASS][:, u * BANK : (u + 1) * BANK], tab[LAST_PASS][:].bitcast(U32).indirect(entries(idx, u * BANK, BANK)))
 
-        h_slot = [0, 1, 2, 3, 0, 1, 4, 5]
-        h_banks = [(0, 1), (2, 3), (0, 1), (2, 4), (0, 1), (2, 7), (5, 6), (0, 3)]
+        h_banks = [(0, 1), (2, 3), (0, 4), (2, 3), (0, 1), (2, 7), (5, 6), (0, 3)]
+        h_tags = {(4, 1): "slot0", (6, 1): "slot1"}
         h = {}
 
         def make_h(c, codes, scales):
-            h[c] = sb([P, S], F32, "h%d" % c, "slot%d" % h_slot[c])
+            if c < 2:
+                whole = sb([P, S], F32, "h%d" % c, "slot%d" % c)
+                h[c] = [whole[:, :BANK], whole[:, BANK:]]
+            else:
+                h[c] = [sb([P, BANK], F32, "h%d_%d" % (c, u), h_tags.get((c, u)))[:] for u in range(2)]
             for u in range(2):
                 cols = slice(u * BANK, (u + 1) * BANK)
                 acc = bank(h_banks[c][u], [P, BANK], F32, "h_acc%d_%d" % (c, u))
@@ -149,148 +164,156 @@ def tile_list_tract_seed_filter_kernel(tc, tab_words, tab_scales, offs, offs2, o
                         rhs=v_words[a][:, cols].bitcast(FP8X4),
                         rhs_scale=v_sc[4 * a :, cols],
                         start=(a == 0),
-                        stop=(a == last),
+                        stop=(a == LAST_PASS),
                     )
-                nc.scalar.copy(h[c][:, cols], acc[:])
+                nc.scalar.copy(h[c][u], acc[:])
 
-        def make_h_nat(c):
-            n = min(c, 2)
-            first = c * P - chunks[n][0]
-            make_h(c, lambda a: w_codes[n][:, a, first : first + P], lambda a: w_sc[n][:, a, first : first + P])
+        def make_h_low(c):
+            n = min(c, len(LOW_CHUNKS) - 1)
+            first = c * P - LOW_CHUNKS[n][0]
+            make_h(c, lambda a: low_codes[n][:, a, first : first + P], lambda a: low_sc[n][:, a, first : first + P])
 
-        def scatter(c, weights, pieces):
-            width = S // pieces
-            for u in range(pieces):
-                cols = slice(u * width, (u + 1) * width)
-                nc.vector.tensor_tensor(pages[c][:].indirect(idx2[:, u * width // 16 : (u + 1) * width // 16]), h[c][:, cols], weights[:, cols], MULT)
+        def scatter(c, u, weights):
+            nc.vector.tensor_tensor(pages[c][:].indirect(entries(idx2, u * BANK, BANK)), h[c][u], weights[:, u * BANK : (u + 1) * BANK], MULT)
 
+        x_tags = ["low_sc0"] + ["h%d_0" % (c + 1) for c in range(1, LAST_TILE)] + ["h2_0"]
+        act_tags = ["raw0_0", "big0", "raw0_2", "raw1_0", "raw1_1", "raw1_2", "raw1_1", "raw1_2"]
         act = {}
-        x_tag = ["w_sc0", "slot0", "x0", "x1", "x0", "x1", "x0", "x1"]
-        act_tag = ["raw0_0", "big0", "raw0_2", "raw1_0", "raw1_1", "raw1_2", "raw1_1", "raw1_2"]
+
+        def by_seed(c, seeds):
+            return act[c][:, :, seeds.start // PACK : seeds.stop // PACK].rearrange("p i q -> p q i")
+
+        every_seed = slice(0, SEEDS)
 
         def fetch(c, pieces=1):
-            x = sb([P, SEEDS], F32, "x%d" % c, x_tag[c])
-            act[c] = sb([P, SEEDS], F32, "act%d" % c, act_tag[c])
+            x = sb([P, SEEDS], F32, "x%d" % c, x_tags[c])
+            act[c] = sb([P, PACK, P], F32, "act%d" % c, act_tags[c])
             width = SEEDS // pieces
             for u in range(pieces):
-                cols = slice(u * width, (u + 1) * width)
-                nc.vector.tensor_copy(x[:, cols], pages[c][:].indirect(idx3[:, u * width // 16 : (u + 1) * width // 16]))
-                nc.scalar.activation(act[c][:, cols], x[:, cols], TANH)
+                seeds = slice(u * width, (u + 1) * width)
+                nc.vector.tensor_copy(x[:, seeds], pages[c][:].indirect(entries(idx3, u * width, width)))
+                nc.scalar.activation(by_seed(c, seeds), x[:, seeds].rearrange("p (q i) -> p q i", i=PACK), TANH)
 
-        zl_t = sb([P, 4, K_PASS], BF16, "zl_t")
+        zl_turned = sb([P, SEEDS // P, K_PASS], BF16, "zl_turned")
 
         def turn_zl(c):
-            scaled = sb([P, SEEDS], BF16, "scaled%d" % c, "scaled%d" % (c % 2))
-            nc.scalar.activation(scaled[:], act[c][:], COPY, scale=gain_nat[:, c : c + 1])
-            turned = bank(4, [P, 4, P], BF16, "turned%d" % c)
-            for m in range(4):
-                nc.tensor.transpose(turned[:, m, :], scaled[:, m * P : (m + 1) * P], ident16[:])
-            nc.scalar.copy(zl_t[:, :, c * P : (c + 1) * P], turned[:])
+            scaled = sb([P, SEEDS], BF16, "scaled%d" % c, "scaled%d" % min(c, 1 + c % 2))
+            nc.scalar.activation(scaled[:].rearrange("p (q i) -> p q i", i=PACK), by_seed(c, every_seed), COPY, scale=gain_low[:, c : c + 1])
+            turned = bank(4, [P, SEEDS // P, P], BF16, "turned%d" % c)
+            for b in range(SEEDS // P):
+                nc.tensor.transpose(turned[:, b, :], scaled[:, b * P : (b + 1) * P], ident16[:])
+            nc.scalar.copy(zl_turned[:, :, c * P : (c + 1) * P], turned[:])
 
-        make_h_nat(0)
-        scatter(0, wgs_nat, 2)
-        later_codes = sb([P, K_PASSES * 3 * P], U32, "later_codes", "slot0")
-        quantize_chunk(1, later_codes[:, : K_PASSES * P].rearrange("p (a c) -> p a c", a=K_PASSES), "first_codes")
-        quantize_chunk(2, later_codes[:, K_PASSES * P :].rearrange("p (a c) -> p a c", a=K_PASSES), "w_sc0")
-        make_h_nat(1)
+        make_h_low(0)
+        scatter(0, 0, wgs_low)
+        scatter(0, 1, wgs_low)
+        later_codes = sb([P, K_PASSES * (K_PASS - P)], U32, "later_codes", "slot0")
+        quantize_low_chunk(1, later_codes[:, : K_PASSES * P].rearrange("p (a c) -> p a c", a=K_PASSES), "first_codes")
+        quantize_low_chunk(2, later_codes[:, K_PASSES * P :].rearrange("p (a c) -> p a c", a=K_PASSES), "low_sc0")
+        make_h_low(1)
         fetch(0)
-        make_h_nat(2)
-        make_h_nat(3)
+        make_h_low(2)
+        make_h_low(3)
         turn_zl(0)
 
-        raw_a = sb([P, PACK, K_PASS], F32, "raw_a", "big0")
+        raw_a = sb([P, 2, PACK, K_PASS], F32, "raw_a", "big0")
         raw_b = sb([P, 2, PACK, K_PASS], F32, "raw_b", "big1")
-        raw_mix = sb([P, PACK, SEEDS], F32, "raw_mix")
-        raw_hi = [raw_a[:], raw_b[:, 0], raw_b[:, 1]]
-        hi_cols = slice(K_PASS, H)
-        load_rows4(raw_hi[0], w1, 0, hi_cols)
-        load_rows4(raw_hi[1], w1, 1, hi_cols)
-        load_rows4(raw_hi[2], w1, 2, hi_cols)
+        high_raw = [raw_a[:, 0], raw_a[:, 1], raw_b[:, 0]]
+        mix_raw = raw_b[:, 1]
+        high_cols = slice(K_PASS, H)
+        load_pass_rows(high_raw[0], w1, 0, high_cols)
         load_page(2)
-        load_rows4(raw_mix[:], mix, 0, slice(0, SEEDS))
-        wgs_mx = sb([P, PACK, S], F32, "wgs_mx", "big2")
-        for g in range(4):
-            nc.sync.dma_start(wgs_mx[32 * g : 32 * (g + 1), :, :], wgs.rearrange("(q t) j -> q t j", t=PACK))
+        load_pass_rows(high_raw[1], w1, 1, high_cols)
+        load_pass_rows(high_raw[2], w1, 2, high_cols)
         load_page(3)
-
-        hi_grouped = {}
-
-        def group_hi(a):
-            hi_grouped[a] = sb([P, PACK, P, PACK], BF16, "hi_grp%d" % a)
-            nc.scalar.copy(hi_grouped[a][:].rearrange("p t m j -> p m j t"), raw_hi[a].rearrange("p j (m t) -> p m j t", t=PACK))
-
-        hi_sc = sb([P, K_PASSES, K_PASS], U8, "hi_sc")
-        scatter(1, wgs_nat, 2)
-        group_hi(0)
-        fetch(1)
-        group_hi(1)
-        group_hi(2)
-        turn_zl(1)
-        scatter(2, wgs_nat, 1)
-        hi_codes = sb([P, K_PASSES, K_PASS], U32, "hi_codes", "slot2")
-        for a in range(K_PASSES):
-            quantize(hi_codes[:, a, :], hi_sc[:, a, :], hi_grouped[a][:].rearrange("p t m j -> p (t m j)"))
-        fetch(2)
-        turn_zl(2)
-        scatter(3, wgs_nat, 1)
-
-        def make_h_mx(c):
-            t = c - 4
-            make_h(c, lambda a: hi_codes[:, a, t * P : (t + 1) * P], lambda a: hi_sc[:, a, t * P : (t + 1) * P])
-
-        load_page(4)
+        load_pass_rows(mix_raw, mix, 0, every_seed)
         wl_w = sb([P, 2, 2 * H], U8, "wl_w")
         nc.sync.dma_start(wl_w[:].bitcast(I32), wl_words.rearrange("a p c -> p a c").bitcast(I32))
-        for q in range(4):
+        for q in range(QUADRANTS):
             nc.sync.dma_start(wl_sc[32 * q : 32 * q + 4, :, :].bitcast(I32), wl_scales[:, 4 * q : 4 * q + 4, :].rearrange("a r c -> r a c").bitcast(I32))
-        load_page(5)
-        load_page(6)
-        load_page(7)
 
-        for c in range(4, 8):
-            make_h_mx(c)
+        span = K_PASS * PACK
+        high_grouped = sb([P, K_PASSES * span], BF16, "high_grouped", "scaled0")
+        high_sc = sb([P, K_PASSES, K_PASS], U8, "high_sc")
+        scatter(1, 0, wgs_low)
+        scatter(1, 1, wgs_low)
+        for a in range(K_PASSES):
+            nc.scalar.copy(
+                high_grouped[:, a * span : (a + 1) * span].rearrange("p (t m i) -> p m i t", t=PACK, i=PACK),
+                high_raw[a].rearrange("p i (m t) -> p m i t", t=PACK),
+            )
+        scatter(2, 0, wgs_low)
+        fetch(1)
+        scatter(2, 1, wgs_low)
+        turn_zl(1)
+        high_codes = sb([P, K_PASSES, K_PASS], U32, "high_codes", "h2_1")
+        for a in range(K_PASSES):
+            quantize(high_codes[:, a, :], high_sc[:, a, :], high_grouped[:, a * span : (a + 1) * span])
+        scatter(3, 0, wgs_low)
+        fetch(2)
+        scatter(3, 1, wgs_low)
+
+        def make_h_high(c):
+            cols = slice((c - LOW_TILES) * P, (c - LOW_TILES + 1) * P)
+            make_h(c, lambda a: high_codes[:, a, cols], lambda a: high_sc[:, a, cols])
+
+        wgs_high = sb([P, PACK, S], F32, "wgs_high", "big2")
+        for t in range(PACK):
+            for q in range(QUADRANTS):
+                nc.sync.dma_start(wgs_high[32 * q : 32 * (q + 1), t, :], wgs.rearrange("(w t) j -> w t j", t=PACK)[:, t, :])
+            load_page(LOW_TILES + t)
+
+        for c in range(LOW_TILES, ROW_TILES):
+            make_h_high(c)
+        turn_zl(2)
+        mix_grouped = sb([P, SEEDS, PACK], BF16, "mix_grouped", "scaled0")
+        interleave(mix_grouped[:], mix_raw)
+        scatter(4, 0, wgs_high[:, 0, :])
         fetch(3)
+        scatter(4, 1, wgs_high[:, 0, :])
+        mix_codes = sb([P, SEEDS], U32, "mix_codes", "slot0")
+        mix_sc = sb([P, SEEDS], U8, "mix_sc")
+        quantize(mix_codes[:], mix_sc[:], mix_grouped[:].rearrange("p m i -> p (m i)"))
         turn_zl(3)
-        zl0 = sb([P, SEEDS, PACK], BF16, "zl0", "raw2_0")
-        zl0_words = zl0[:].rearrange("p m j -> p (m j)").bitcast(F32)
+
+        zl_low = sb([P, SEEDS, PACK], BF16, "zl_low", "raw2_0")
+        zl_low_words = zl_low[:].rearrange("p m i -> p (m i)").bitcast(F32)
         for half in range(2):
             back = bank(5 + half, [P, 2, 2, P], F32, "back%d" % half)
-            for m in range(2):
-                words = zl_t[:, 2 * half + m, :].bitcast(F32)
+            for b in range(2):
+                words = zl_turned[:, 2 * half + b, :].bitcast(F32)
                 for u in range(2):
-                    nc.tensor.transpose(back[:, m, u, :], words[:, u : 2 * P : 2], ident32[:])
+                    nc.tensor.transpose(back[:, b, u, :], words[:, u : 2 * P : 2], ident32[:])
             nc.scalar.copy(
-                zl0_words[:, half * BANK : (half + 1) * BANK].rearrange("p (a m u) -> p a m u", a=2, u=2),
-                back[:].rearrange("p a u m -> p a m u"),
+                zl_low_words[:, half * BANK : (half + 1) * BANK].rearrange("p (b m u) -> p b m u", b=2, u=2),
+                back[:].rearrange("p b u m -> p b m u"),
             )
-        mix_grouped = sb([P, SEEDS, PACK], BF16, "mix_grp", "hi_grp1")
-        interleave(mix_grouped[:], raw_mix[:])
 
-        zr0_planes = sb([P, PACK, K_PASS], BF16, "zr0_planes", "slot3")
+        zr_low_planes = sb([P, PACK, K_PASS], BF16, "zr_low_planes", "h2_1")
         for i in range(PACK):
-            turned = bank(7, [P, 4, P], F32, "zr0_turned%d" % i)
-            for c in range(4):
-                nc.tensor.transpose(turned[:, c, :], act[c][:, i:SEEDS:PACK], ident32[:])
-            nc.scalar.activation(zr0_planes[:, i, :], turned[:].rearrange("p c r -> p (c r)"), COPY, scale=seed_mx[:, i : i + 1])
-        zr0 = sb([P, K_PASS, PACK], BF16, "zr0", "raw2_1")
-        interleave(zr0[:], zr0_planes[:])
+            turned = bank(7, [P, LOW_TILES, P], F32, "zr_low_turned%d" % i)
+            for c in range(LOW_TILES):
+                nc.tensor.transpose(turned[:, c, :], act[c][:, i, :], ident32[:])
+            nc.scalar.activation(zr_low_planes[:, i, :], turned[:].rearrange("q c p -> q (c p)"), COPY, scale=seed_w[:, i : i + 1])
+        zr_low = sb([P, K_PASS, PACK], BF16, "zr_low", "raw2_1")
+        interleave(zr_low[:], zr_low_planes[:])
 
-        zl1 = sb([P, SEEDS, PACK], BF16, "zl1")
-        zr1 = sb([P, K_PASS, PACK], BF16, "zr1")
+        zl_high = sb([P, SEEDS, PACK], BF16, "zl_high")
+        zr_high = sb([P, K_PASS, PACK], BF16, "zr_high")
 
         def finish_zr(c):
-            t = c - 4
-            turned = bank(7, [P, PACK, P], F32, "zr1_turned%d" % t)
-            planes = sb([P, PACK, P], BF16, "zr1_planes%d" % t, "scaled%d" % (t % 2))
+            t = c - LOW_TILES
+            turned = bank(7, [P, PACK, P], F32, "zr_high_turned%d" % t)
+            planes = sb([P, PACK, P], BF16, "zr_high_planes%d" % t, "scaled%d" % (1 + t % 2))
             for i in range(PACK):
-                nc.tensor.transpose(turned[:, i, :], act[c][:, i:SEEDS:PACK], ident32[:])
+                nc.tensor.transpose(turned[:, i, :], act[c][:, i, :], ident32[:])
             for i in range(PACK):
-                nc.scalar.activation(planes[:, i, :], turned[:, i, :], COPY, scale=seed_mx[:, i : i + 1])
-            nc.scalar.copy(zr1[:].rearrange("q (p t) i -> q t p i", t=PACK)[:, t], planes[:].rearrange("q i p -> q p i"))
+                nc.scalar.activation(planes[:, i, :], turned[:, i, :], COPY, scale=seed_w[:, i : i + 1])
+            nc.scalar.copy(zr_high[:].rearrange("q (p t) i -> q t p i", t=PACK)[:, t], planes[:].rearrange("q i p -> q p i"))
 
         def finish_zl(c):
-            t = c - 4
-            nc.scalar.activation(zl1[:, :, t], act[c][:], COPY, scale=gain_mx[:, t : t + 1])
+            t = c - LOW_TILES
+            nc.scalar.activation(zl_high[:, :, t].rearrange("p (q i) -> p q i", i=PACK), by_seed(c, every_seed), COPY, scale=gain_high[:, t : t + 1])
 
         acc_out = {}
 
@@ -306,70 +329,69 @@ def tile_list_tract_seed_filter_kernel(tc, tab_words, tab_scales, offs, offs2, o
             )
 
         def right_pass(n, codes, scales, stop):
-            cols = slice((n % 4) * P, (n % 4 + 1) * P)
+            cols = slice((n % LOW_TILES) * P, (n % LOW_TILES + 1) * P)
             nc.tensor.matmul_mx(
                 out=acc_out[n][:],
                 lhsT=codes[:, cols].bitcast(FP8X4),
                 lhsT_scale=scales[:, cols],
-                rhs=early_codes[:, 1, :].bitcast(FP8X4),
-                rhs_scale=early_sc[:, 1, :],
+                rhs=mix_codes[:].bitcast(FP8X4),
+                rhs_scale=mix_sc[:],
                 start=False,
                 stop=stop,
             )
 
-        scatter(4, wgs_mx[:, 0, :], 1)
+        scatter(5, 0, wgs_high[:, 1, :])
         fetch(4)
+        scatter(5, 1, wgs_high[:, 1, :])
+        zl_low_codes = sb([P, SEEDS], U32, "zl_low_codes", "h5_1")
+        zl_low_sc = sb([P, SEEDS], U8, "zl_low_sc")
+        quantize(zl_low_codes[:], zl_low_sc[:], zl_low[:].rearrange("p m i -> p (m i)"))
         finish_zl(4)
         finish_zr(4)
-        scatter(5, wgs_mx[:, 1, :], 1)
-        early_codes = sb([P, 2, SEEDS], U32, "early_codes", "slot1")
-        early_sc = sb([P, 2, SEEDS], U8, "early_sc")
-        quantize(early_codes[:, 0, :], early_sc[:, 0, :], zl0[:].rearrange("p m j -> p (m j)"))
-        quantize(early_codes[:, 1, :], early_sc[:, 1, :], mix_grouped[:].rearrange("p m j -> p (m j)"))
-        fetch(5)
-        finish_zl(5)
-        finish_zr(5)
-        for n in range(7):
+        for n in range(LAST_TILE):
             acc_out[n] = bank(n, [P, SEEDS], F32, "acc_out%d" % n)
-            left_pass(n, 0, early_codes[:, 0, :], early_sc[:, 0, :], True, False)
-        scatter(6, wgs_mx[:, 2, :], 1)
-        fetch(6)
-        finish_zl(6)
-        finish_zr(6)
-        scatter(7, wgs_mx[:, 3, :], 1)
-        zr0_codes = sb([P, K_PASS], U32, "zr0_codes", "slot5")
-        zr0_sc = sb([P, K_PASS], U8, "zr0_sc")
-        quantize(zr0_codes[:], zr0_sc[:], zr0[:].rearrange("p n i -> p (n i)"))
-        fetch(7, 2)
-        for n in range(4):
-            right_pass(n, zr0_codes, zr0_sc, False)
-        for u in range(2):
-            cols = slice(u * SEEDS // 2, (u + 1) * SEEDS // 2)
-            nc.vector.tensor_scalar(zl1[:, cols, 3], act[7][:, cols], gain_mx[:, 3:4], None, MULT)
-        zl1_codes = sb([P, SEEDS], U32, "zl1_codes")
-        zl1_sc = sb([P, SEEDS], U8, "zl1_sc")
-        quantize(zl1_codes[:], zl1_sc[:], zl1[:].rearrange("p m j -> p (m j)"))
-        finish_zr(7)
-        zr1_codes = sb([P, K_PASS], U32, "zr1_codes")
-        zr1_sc = sb([P, K_PASS], U8, "zr1_sc")
-        quantize(zr1_codes[:], zr1_sc[:], zr1[:].rearrange("p n i -> p (n i)"))
+            left_pass(n, 0, zl_low_codes[:], zl_low_sc[:], True, False)
+        for c in range(5, LAST_TILE):
+            scatter(c + 1, 0, wgs_high[:, c + 1 - LOW_TILES, :])
+            fetch(c)
+            scatter(c + 1, 1, wgs_high[:, c + 1 - LOW_TILES, :])
+            finish_zl(c)
+            finish_zr(c)
+        zr_low_codes = sb([P, K_PASS], U32, "zr_low_codes", "h7_1")
+        zr_low_sc = sb([P, K_PASS], U8, "zr_low_sc")
+        quantize(zr_low_codes[:], zr_low_sc[:], zr_low[:].rearrange("q n i -> q (n i)"))
 
-        staged = sb([P, 8, SEEDS], F32, "staged", "big0")
+        fetch(LAST_TILE, 2)
+        for n in range(LOW_TILES):
+            right_pass(n, zr_low_codes, zr_low_sc, False)
+        for u in range(2):
+            seeds = slice(u * SEEDS // 2, (u + 1) * SEEDS // 2)
+            nc.vector.tensor_scalar(zl_high[:, seeds, PACK - 1].rearrange("p (q i) -> p q i", i=PACK), by_seed(LAST_TILE, seeds), gain_high[:, PACK - 1 : PACK], None, MULT)
+        zl_high_codes = sb([P, SEEDS], U32, "zl_high_codes")
+        zl_high_sc = sb([P, SEEDS], U8, "zl_high_sc")
+        quantize(zl_high_codes[:], zl_high_sc[:], zl_high[:].rearrange("p m i -> p (m i)"))
+        finish_zr(LAST_TILE)
+        zr_high_codes = sb([P, K_PASS], U32, "zr_high_codes")
+        zr_high_sc = sb([P, K_PASS], U8, "zr_high_sc")
+        quantize(zr_high_codes[:], zr_high_sc[:], zr_high[:].rearrange("q n i -> q (n i)"))
+
+        staged = sb([P, ROW_TILES, SEEDS], F32, "staged", "big0")
+        emptied_by_scalar = (2, 3, 5, 7)
 
         def hand_out(n):
-            if n in (2, 3, 5, 7):
+            if n in emptied_by_scalar:
                 nc.scalar.copy(staged[:, n, :], acc_out[n][:])
             else:
                 nc.vector.tensor_copy(staged[:, n, :], acc_out[n][:])
             nc.sync.dma_start(out[n * P : (n + 1) * P, :], staged[:, n, :])
 
-        for n in range(7):
-            left_pass(n, 1, zl1_codes[:], zl1_sc[:], False, n < 4)
-            if n < 4:
+        for n in range(LAST_TILE):
+            left_pass(n, 1, zl_high_codes[:], zl_high_sc[:], False, n < LOW_TILES)
+            if n < LOW_TILES:
                 hand_out(n)
-        acc_out[7] = bank(7, [P, SEEDS], F32, "acc_out7")
-        left_pass(7, 0, early_codes[:, 0, :], early_sc[:, 0, :], True, False)
-        left_pass(7, 1, zl1_codes[:], zl1_sc[:], False, False)
-        for n in range(4, 8):
-            right_pass(n, zr1_codes, zr1_sc, True)
+        acc_out[LAST_TILE] = bank(LAST_TILE, [P, SEEDS], F32, "acc_out%d" % LAST_TILE)
+        left_pass(LAST_TILE, 0, zl_low_codes[:], zl_low_sc[:], True, False)
+        left_pass(LAST_TILE, 1, zl_high_codes[:], zl_high_sc[:], False, False)
+        for n in range(LOW_TILES, ROW_TILES):
+            right_pass(n, zr_high_codes, zr_high_sc, True)
             hand_out(n)

from contextlib import ExitStack

import concourse.mybir as mybir
from concourse.masks import make_identity

F32 = mybir.dt.float32
BF16 = mybir.dt.bfloat16
I32 = mybir.dt.int32
U32 = mybir.dt.uint32
U16 = mybir.dt.uint16
U8 = mybir.dt.uint8
FP8X4 = mybir.dt.float8_e4m3fn_x4
FP4X4 = mybir.dt.float4_e2m1fn_x4
MULT = mybir.AluOpType.mult
COPY = mybir.ActivationFunctionType.Copy
TANH = mybir.ActivationFunctionType.Tanh

K, H, T, S, T2, SEEDS = 1536, 1024, 4096, 1024, 2048, 512
P = 128
PACK = 4
K_PASS = P * PACK
K_PASSES = K // K_PASS
LAST_PASS = K_PASSES - 1
BANK = 512
LIST_ROWS = 16
QUADRANTS = 4
LOW_TILES = 4
ROW_TILES = H // P
LAST_TILE = ROW_TILES - 1
PAGE_SLOTS = 4
RUN = 4
LOW_CHUNKS = [(0, P), (P, P), (2 * P, 2 * P)]
FLOPS = 2 * K * H * S + 2 * H * H * SEEDS + 2 * SEEDS * H * SEEDS


def tile_list_tract_seed_filter_kernel(tc, tab_words, tab_scales, offs, offs2, offs3, w1, wgs, page0, gain, seedw, wl_words, wl_scales, mix, out):
    nc = tc.nc
    with ExitStack() as ctx:
        lists = ctx.enter_context(tc.tile_pool(name="lists", bufs=1))
        keep = ctx.enter_context(tc.tile_pool(name="keep", bufs=1))
        psum = ctx.enter_context(tc.psum_pool(name="psum", bufs=1))

        def sb(shape, dtype, name, tag=None):
            return keep.tile(shape, dtype, name=name, tag=tag or name, align_bytes=64)

        def bank(number, shape, dtype, name):
            return psum.tile(shape, dtype, name=name, tag="bank%d" % number)

        def entries(list_tile, first, count):
            return list_tile[:, first // LIST_ROWS : (first + count) // LIST_ROWS]

        def load_pass_rows(dst, src, a, cols):
            nc.sync.dma_start(dst, src[a * K_PASS : (a + 1) * K_PASS, cols].rearrange("(p i) c -> p i c", i=PACK))

        def interleave(grouped, planes):
            nc.scalar.copy(grouped.rearrange("p (c n) i -> p c i n", n=RUN), planes.rearrange("p i (c n) -> p c i n", n=RUN))

        def quantize(codes, scales, grouped):
            nc.vector.quantize_mx(out=codes.bitcast(FP8X4), scales=scales, in_=grouped)

        idx = lists.tile([P, S // LIST_ROWS], U16, name="idx")
        idx2 = lists.tile([P, S // LIST_ROWS], U16, name="idx2")
        idx3 = lists.tile([P, SEEDS // LIST_ROWS], U16, name="idx3")

        tab_sc = sb([P, T], U8, "tab_sc")
        nc.vector.memset(tab_sc[:].bitcast(I32), 0)
        for q in range(QUADRANTS):
            nc.gpsimd.dma_start(tab_sc[32 * q : 32 * q + 4 * K_PASSES, :].bitcast(I32), tab_scales[:, 4 * q : 4 * q + 4, :].bitcast(I32))
        wl_sc = sb([P, 2, H], U8, "wl_sc")
        nc.gpsimd.memset(wl_sc[:].bitcast(I32), 0)
        ident32 = sb([P, P], F32, "ident32")
        make_identity(nc, ident32[:])
        ident16 = sb([P, P], BF16, "ident16")
        make_identity(nc, ident16[:])

        tab = [sb([P, T], I32, "tab%d" % a, "big%d" % a) for a in range(K_PASSES)]

        def load_tab(a):
            nc.sync.dma_start(tab[a][:], tab_words[a].rearrange("p t i -> p (t i)").bitcast(I32))

        low_raw = [
            [sb([P, PACK, width], F32, "raw%d_%d" % (n, a), "slot1" if (n, a) == (len(LOW_CHUNKS) - 1, LAST_PASS) else None) for a in range(K_PASSES)]
            for n, (first, width) in enumerate(LOW_CHUNKS)
        ]

        def load_low_chunk(n):
            first, width = LOW_CHUNKS[n]
            for a in range(K_PASSES):
                load_pass_rows(low_raw[n][a][:], w1, a, slice(first, first + width))

        pages = {}

        def load_page(c):
            pages[c] = sb([P, T2], F32, "page%d" % c, "page%d" % (c % PAGE_SLOTS))
            if c < LOW_TILES:
                rows = page0[c * P : (c + 1) * P, :]
            else:
                rows = page0[K_PASS:, :].rearrange("(p t) c -> p t c", t=PACK)[:, c - LOW_TILES, :]
            nc.sync.dma_start(pages[c][:], rows)

        nc.sync.dma_start(idx[:], offs)
        load_tab(0)
        load_tab(1)
        load_low_chunk(0)
        load_tab(2)
        nc.sync.dma_start(idx2[:], offs2)
        wgs_low = sb([P, S], F32, "wgs_low")
        nc.sync.dma_start(wgs_low[:, :BANK], wgs[:, :BANK])
        load_page(0)
        nc.sync.dma_start(wgs_low[:, BANK:], wgs[:, BANK:])
        load_low_chunk(1)
        load_low_chunk(2)
        nc.sync.dma_start(idx3[:], offs3)
        load_page(1)
        gain_low = sb([P, LOW_TILES], F32, "gain_low")
        with nc.allow_non_contiguous_dma(reason="one gain for each partition and low tile"):
            nc.sync.dma_start(gain_low[:], gain[0:K_PASS].rearrange("(c p) -> p c", p=P))
        gain_high = sb([P, PACK], F32, "gain_high")
        nc.sync.dma_start(gain_high[:], gain[K_PASS:].rearrange("(p t) -> p t", t=PACK))
        seed_w = sb([P, PACK], F32, "seed_w")
        nc.sync.dma_start(seed_w[:], seedw.rearrange("(q i) -> q i", i=PACK))

        v_sc = sb([P, S], U8, "v_sc")
        v_words = [sb([P, S], U32, "v_words%d" % a) for a in range(LAST_PASS)]
        nc.vector.tensor_copy(v_words[0][:], tab[0][:].bitcast(U32).indirect(idx[:]))
        nc.vector.tensor_copy(v_sc[:], tab_sc[:].indirect(idx[:]))
        nc.vector.tensor_copy(v_words[1][:], tab[1][:].bitcast(U32).indirect(idx[:]))

        low_sc = [sb([P, K_PASSES, width], U8, "low_sc%d" % n) for n, (first, width) in enumerate(LOW_CHUNKS)]
        low_codes = {}

        def quantize_low_chunk(n, codes, grouped_tag):
            first, width = LOW_CHUNKS[n]
            low_codes[n] = codes
            grouped = sb([P, K_PASSES, width, PACK], BF16, "low_grouped%d" % n, grouped_tag)
            for a in range(K_PASSES):
                interleave(grouped[:, a], low_raw[n][a][:])
                quantize(codes[:, a, :], low_sc[n][:, a, :], grouped[:, a].rearrange("p c i -> p (c i)"))

        first_codes = sb([P, K_PASSES, P], U32, "first_codes")
        quantize_low_chunk(0, first_codes[:], "tab_sc")
        v_words.append(sb([P, S], U32, "v_words%d" % LAST_PASS, "tab_sc"))
        for u in range(2):
            nc.vector.tensor_copy(v_words[LAST_PASS][:, u * BANK : (u + 1) * BANK], tab[LAST_PASS][:].bitcast(U32).indirect(entries(idx, u * BANK, BANK)))

        h_banks = [(0, 1), (2, 3), (0, 4), (2, 3), (0, 1), (2, 7), (5, 6), (0, 3)]
        h_tags = {(4, 1): "slot0", (6, 1): "slot1"}
        h = {}

        def make_h(c, codes, scales):
            if c < 2:
                whole = sb([P, S], F32, "h%d" % c, "slot%d" % c)
                h[c] = [whole[:, :BANK], whole[:, BANK:]]
            else:
                h[c] = [sb([P, BANK], F32, "h%d_%d" % (c, u), h_tags.get((c, u)))[:] for u in range(2)]
            for u in range(2):
                cols = slice(u * BANK, (u + 1) * BANK)
                acc = bank(h_banks[c][u], [P, BANK], F32, "h_acc%d_%d" % (c, u))
                for a in range(K_PASSES):
                    nc.tensor.matmul_mx(
                        out=acc[:],
                        lhsT=codes(a).bitcast(FP8X4),
                        lhsT_scale=scales(a),
                        rhs=v_words[a][:, cols].bitcast(FP8X4),
                        rhs_scale=v_sc[4 * a :, cols],
                        start=(a == 0),
                        stop=(a == LAST_PASS),
                    )
                nc.scalar.copy(h[c][u], acc[:])

        def make_h_low(c):
            n = min(c, len(LOW_CHUNKS) - 1)
            first = c * P - LOW_CHUNKS[n][0]
            make_h(c, lambda a: low_codes[n][:, a, first : first + P], lambda a: low_sc[n][:, a, first : first + P])

        def scatter(c, u, weights):
            nc.vector.tensor_tensor(pages[c][:].indirect(entries(idx2, u * BANK, BANK)), h[c][u], weights[:, u * BANK : (u + 1) * BANK], MULT)

        x_tags = ["low_sc0"] + ["h%d_0" % (c + 1) for c in range(1, LAST_TILE)] + ["h2_0"]
        act_tags = ["raw0_0", "big0", "raw0_2", "raw1_0", "raw1_1", "raw1_2", "raw1_1", "raw1_2"]
        act = {}

        def by_seed(c, seeds):
            return act[c][:, :, seeds.start // PACK : seeds.stop // PACK].rearrange("p i q -> p q i")

        every_seed = slice(0, SEEDS)

        def fetch(c, pieces=1):
            x = sb([P, SEEDS], F32, "x%d" % c, x_tags[c])
            act[c] = sb([P, PACK, P], F32, "act%d" % c, act_tags[c])
            width = SEEDS // pieces
            for u in range(pieces):
                seeds = slice(u * width, (u + 1) * width)
                nc.vector.tensor_copy(x[:, seeds], pages[c][:].indirect(entries(idx3, u * width, width)))
                nc.scalar.activation(by_seed(c, seeds), x[:, seeds].rearrange("p (q i) -> p q i", i=PACK), TANH)

        zl_turned = sb([P, SEEDS // P, K_PASS], BF16, "zl_turned")

        def turn_zl(c):
            scaled = sb([P, SEEDS], BF16, "scaled%d" % c, "scaled%d" % min(c, 1 + c % 2))
            nc.scalar.activation(scaled[:].rearrange("p (q i) -> p q i", i=PACK), by_seed(c, every_seed), COPY, scale=gain_low[:, c : c + 1])
            turned = bank(4, [P, SEEDS // P, P], BF16, "turned%d" % c)
            for b in range(SEEDS // P):
                nc.tensor.transpose(turned[:, b, :], scaled[:, b * P : (b + 1) * P], ident16[:])
            nc.scalar.copy(zl_turned[:, :, c * P : (c + 1) * P], turned[:])

        make_h_low(0)
        scatter(0, 0, wgs_low)
        scatter(0, 1, wgs_low)
        later_codes = sb([P, K_PASSES * (K_PASS - P)], U32, "later_codes", "slot0")
        quantize_low_chunk(1, later_codes[:, : K_PASSES * P].rearrange("p (a c) -> p a c", a=K_PASSES), "first_codes")
        quantize_low_chunk(2, later_codes[:, K_PASSES * P :].rearrange("p (a c) -> p a c", a=K_PASSES), "low_sc0")
        make_h_low(1)
        fetch(0)
        make_h_low(2)
        make_h_low(3)
        turn_zl(0)

        raw_a = sb([P, 2, PACK, K_PASS], F32, "raw_a", "big0")
        raw_b = sb([P, 2, PACK, K_PASS], F32, "raw_b", "big1")
        high_raw = [raw_a[:, 0], raw_a[:, 1], raw_b[:, 0]]
        mix_raw = raw_b[:, 1]
        high_cols = slice(K_PASS, H)
        load_pass_rows(high_raw[0], w1, 0, high_cols)
        load_page(2)
        load_pass_rows(high_raw[1], w1, 1, high_cols)
        load_pass_rows(high_raw[2], w1, 2, high_cols)
        load_page(3)
        load_pass_rows(mix_raw, mix, 0, every_seed)
        wl_w = sb([P, 2, 2 * H], U8, "wl_w")
        nc.sync.dma_start(wl_w[:].bitcast(I32), wl_words.rearrange("a p c -> p a c").bitcast(I32))
        for q in range(QUADRANTS):
            nc.sync.dma_start(wl_sc[32 * q : 32 * q + 4, :, :].bitcast(I32), wl_scales[:, 4 * q : 4 * q + 4, :].rearrange("a r c -> r a c").bitcast(I32))

        span = K_PASS * PACK
        high_grouped = sb([P, K_PASSES * span], BF16, "high_grouped", "scaled0")
        high_sc = sb([P, K_PASSES, K_PASS], U8, "high_sc")
        scatter(1, 0, wgs_low)
        scatter(1, 1, wgs_low)
        for a in range(K_PASSES):
            nc.scalar.copy(
                high_grouped[:, a * span : (a + 1) * span].rearrange("p (t m i) -> p m i t", t=PACK, i=PACK),
                high_raw[a].rearrange("p i (m t) -> p m i t", t=PACK),
            )
        scatter(2, 0, wgs_low)
        fetch(1)
        scatter(2, 1, wgs_low)
        turn_zl(1)
        high_codes = sb([P, K_PASSES, K_PASS], U32, "high_codes", "h2_1")
        for a in range(K_PASSES):
            quantize(high_codes[:, a, :], high_sc[:, a, :], high_grouped[:, a * span : (a + 1) * span])
        scatter(3, 0, wgs_low)
        fetch(2)
        scatter(3, 1, wgs_low)

        def make_h_high(c):
            cols = slice((c - LOW_TILES) * P, (c - LOW_TILES + 1) * P)
            make_h(c, lambda a: high_codes[:, a, cols], lambda a: high_sc[:, a, cols])

        wgs_high = sb([P, PACK, S], F32, "wgs_high", "big2")
        for t in range(PACK):
            for q in range(QUADRANTS):
                nc.sync.dma_start(wgs_high[32 * q : 32 * (q + 1), t, :], wgs.rearrange("(w t) j -> w t j", t=PACK)[:, t, :])
            load_page(LOW_TILES + t)

        for c in range(LOW_TILES, ROW_TILES):
            make_h_high(c)
        turn_zl(2)
        mix_grouped = sb([P, SEEDS, PACK], BF16, "mix_grouped", "scaled0")
        interleave(mix_grouped[:], mix_raw)
        scatter(4, 0, wgs_high[:, 0, :])
        fetch(3)
        scatter(4, 1, wgs_high[:, 0, :])
        mix_codes = sb([P, SEEDS], U32, "mix_codes", "slot0")
        mix_sc = sb([P, SEEDS], U8, "mix_sc")
        quantize(mix_codes[:], mix_sc[:], mix_grouped[:].rearrange("p m i -> p (m i)"))
        turn_zl(3)

        zl_low = sb([P, SEEDS, PACK], BF16, "zl_low", "raw2_0")
        zl_low_words = zl_low[:].rearrange("p m i -> p (m i)").bitcast(F32)
        for half in range(2):
            back = bank(5 + half, [P, 2, 2, P], F32, "back%d" % half)
            for b in range(2):
                words = zl_turned[:, 2 * half + b, :].bitcast(F32)
                for u in range(2):
                    nc.tensor.transpose(back[:, b, u, :], words[:, u : 2 * P : 2], ident32[:])
            nc.scalar.copy(
                zl_low_words[:, half * BANK : (half + 1) * BANK].rearrange("p (b m u) -> p b m u", b=2, u=2),
                back[:].rearrange("p b u m -> p b m u"),
            )

        zr_low_planes = sb([P, PACK, K_PASS], BF16, "zr_low_planes", "h2_1")
        for i in range(PACK):
            turned = bank(7, [P, LOW_TILES, P], F32, "zr_low_turned%d" % i)
            for c in range(LOW_TILES):
                nc.tensor.transpose(turned[:, c, :], act[c][:, i, :], ident32[:])
            nc.scalar.activation(zr_low_planes[:, i, :], turned[:].rearrange("q c p -> q (c p)"), COPY, scale=seed_w[:, i : i + 1])
        zr_low = sb([P, K_PASS, PACK], BF16, "zr_low", "raw2_1")
        interleave(zr_low[:], zr_low_planes[:])

        zl_high = sb([P, SEEDS, PACK], BF16, "zl_high")
        zr_high = sb([P, K_PASS, PACK], BF16, "zr_high")

        def finish_zr(c):
            t = c - LOW_TILES
            turned = bank(7, [P, PACK, P], F32, "zr_high_turned%d" % t)
            planes = sb([P, PACK, P], BF16, "zr_high_planes%d" % t, "scaled%d" % (1 + t % 2))
            for i in range(PACK):
                nc.tensor.transpose(turned[:, i, :], act[c][:, i, :], ident32[:])
            for i in range(PACK):
                nc.scalar.activation(planes[:, i, :], turned[:, i, :], COPY, scale=seed_w[:, i : i + 1])
            nc.scalar.copy(zr_high[:].rearrange("q (p t) i -> q t p i", t=PACK)[:, t], planes[:].rearrange("q i p -> q p i"))

        def finish_zl(c):
            t = c - LOW_TILES
            nc.scalar.activation(zl_high[:, :, t].rearrange("p (q i) -> p q i", i=PACK), by_seed(c, every_seed), COPY, scale=gain_high[:, t : t + 1])

        acc_out = {}

        def left_pass(n, a, codes, scales, start, stop):
            nc.tensor.matmul_mx(
                out=acc_out[n][:],
                lhsT=wl_w[:, a, 2 * n * P : 2 * (n + 1) * P].bitcast(FP4X4),
                lhsT_scale=wl_sc[:, a, n * P : (n + 1) * P],
                rhs=codes.bitcast(FP8X4),
                rhs_scale=scales,
                start=start,
                stop=stop,
            )

        def right_pass(n, codes, scales, stop):
            cols = slice((n % LOW_TILES) * P, (n % LOW_TILES + 1) * P)
            nc.tensor.matmul_mx(
                out=acc_out[n][:],
                lhsT=codes[:, cols].bitcast(FP8X4),
                lhsT_scale=scales[:, cols],
                rhs=mix_codes[:].bitcast(FP8X4),
                rhs_scale=mix_sc[:],
                start=False,
                stop=stop,
            )

        scatter(5, 0, wgs_high[:, 1, :])
        fetch(4)
        scatter(5, 1, wgs_high[:, 1, :])
        zl_low_codes = sb([P, SEEDS], U32, "zl_low_codes", "h5_1")
        zl_low_sc = sb([P, SEEDS], U8, "zl_low_sc")
        quantize(zl_low_codes[:], zl_low_sc[:], zl_low[:].rearrange("p m i -> p (m i)"))
        finish_zl(4)
        finish_zr(4)
        for n in range(LAST_TILE):
            acc_out[n] = bank(n, [P, SEEDS], F32, "acc_out%d" % n)
            left_pass(n, 0, zl_low_codes[:], zl_low_sc[:], True, False)
        for c in range(5, LAST_TILE):
            scatter(c + 1, 0, wgs_high[:, c + 1 - LOW_TILES, :])
            fetch(c)
            scatter(c + 1, 1, wgs_high[:, c + 1 - LOW_TILES, :])
            finish_zl(c)
            finish_zr(c)
        zr_low_codes = sb([P, K_PASS], U32, "zr_low_codes", "h7_1")
        zr_low_sc = sb([P, K_PASS], U8, "zr_low_sc")
        quantize(zr_low_codes[:], zr_low_sc[:], zr_low[:].rearrange("q n i -> q (n i)"))

        fetch(LAST_TILE, 2)
        for n in range(LOW_TILES):
            right_pass(n, zr_low_codes, zr_low_sc, False)
        for u in range(2):
            seeds = slice(u * SEEDS // 2, (u + 1) * SEEDS // 2)
            nc.vector.tensor_scalar(zl_high[:, seeds, PACK - 1].rearrange("p (q i) -> p q i", i=PACK), by_seed(LAST_TILE, seeds), gain_high[:, PACK - 1 : PACK], None, MULT)
        zl_high_codes = sb([P, SEEDS], U32, "zl_high_codes")
        zl_high_sc = sb([P, SEEDS], U8, "zl_high_sc")
        quantize(zl_high_codes[:], zl_high_sc[:], zl_high[:].rearrange("p m i -> p (m i)"))
        finish_zr(LAST_TILE)
        zr_high_codes = sb([P, K_PASS], U32, "zr_high_codes")
        zr_high_sc = sb([P, K_PASS], U8, "zr_high_sc")
        quantize(zr_high_codes[:], zr_high_sc[:], zr_high[:].rearrange("q n i -> q (n i)"))

        staged = sb([P, ROW_TILES, SEEDS], F32, "staged", "big0")
        emptied_by_scalar = (2, 3, 5, 7)

        def hand_out(n):
            if n in emptied_by_scalar:
                nc.scalar.copy(staged[:, n, :], acc_out[n][:])
            else:
                nc.vector.tensor_copy(staged[:, n, :], acc_out[n][:])
            nc.sync.dma_start(out[n * P : (n + 1) * P, :], staged[:, n, :])

        for n in range(LAST_TILE):
            left_pass(n, 1, zl_high_codes[:], zl_high_sc[:], False, n < LOW_TILES)
            if n < LOW_TILES:
                hand_out(n)
        acc_out[LAST_TILE] = bank(LAST_TILE, [P, SEEDS], F32, "acc_out%d" % LAST_TILE)
        left_pass(LAST_TILE, 0, zl_low_codes[:], zl_low_sc[:], True, False)
        left_pass(LAST_TILE, 1, zl_high_codes[:], zl_high_sc[:], False, False)
        for n in range(LOW_TILES, ROW_TILES):
            right_pass(n, zr_high_codes, zr_high_sc, True)
            hand_out(n)
